import numpy as np
import ml_dtypes


def mxq(x, axis, fmt="e4m3"):
    dtype, down = {"e4m3": (ml_dtypes.float8_e4m3fn, 7), "e5m2": (ml_dtypes.float8_e5m2, 14)}[fmt]
    v = np.moveaxis(np.asarray(x, np.float32).astype(ml_dtypes.bfloat16).astype(np.float64), axis, -1)
    blocks = v.reshape(v.shape[:-1] + (-1, 32))
    amax = np.abs(blocks).max(-1, keepdims=True)
    byte = np.maximum(np.where(amax > 0, np.frexp(amax)[1] - 1 + 127, 0) - down, 1)
    scale = np.exp2(byte - 127.0)
    codes = (blocks / scale).astype(np.float32).astype(dtype).astype(np.float64)
    return np.moveaxis((codes * scale).reshape(v.shape), -1, axis)


WIDE = False


def mx_kscale(k):
    if not WIDE:
        return np.ones(k)
    levels = np.array([18, -18])
    if k % 512:
        return np.exp2(np.random.permutation(np.resize(levels, k // 32))).repeat(32)
    a = np.empty((k // 512, 16))
    for p in range(k // 512):
        a[p, :8] = np.random.permutation(np.resize(levels, 8))
        for g in range(8):
            far = levels[np.abs(levels - a[p, g]) >= 10]
            a[p, g + 8] = far[np.random.randint(len(far))]
    return np.exp2(a.ravel()).repeat(32)


def f64(x):
    return np.asarray(x).astype(np.float64)


def striped(idx):
    return np.tile(np.asarray(idx).reshape(-1, 16).T, (8, 1)).astype(np.uint16)


def unstriped(offs):
    return offs[:16].T.reshape(-1).astype(np.int64)


def setup_inputs():
    n = np.random.standard_normal
    uni = np.random.uniform
    dst = np.random.permutation(np.repeat(np.arange(1024), 2))
    inn = np.argsort(dst, kind="stable")
    lea = np.random.permutation(2048)
    f_m = mx_kscale(512)
    return {
        "dyT": (np.round(n((512, 1024)) * 8) / 8 * f_m[:, None]).astype(np.float32),
        "hE": (np.round(1.0 / (1.0 + np.exp(-3.0 * n((512, 2048)))) * 256) / 256).astype(np.float32),
        "ws": (n((512, 512)) / np.sqrt(512) / f_m[:, None]).astype(np.float32),
        "wtt": (n((512, 512)) / np.sqrt(512) / f_m[:, None]).astype(np.float32),
        "dstoffs": striped(dst),
        "innoffs": striped(inn),
        "leaoffs": striped(lea),
    }


def reference(dyT, hE, ws, wtt, dstoffs, innoffs, leaoffs):
    dst = unstriped(dstoffs)
    inn = unstriped(innoffs)
    lea = unstriped(leaoffs)
    dyT_c = f64(dyT)[:, dst]
    dz = dyT_c * f64(hE) * (1.0 - f64(hE))
    q_dz = mxq(dz, 0, "e5m2")
    u = mxq(f64(ws), 0, "e4m3").T @ q_dz
    v = mxq(f64(wtt), 0, "e4m3").T @ q_dz
    u_yo = u[:, lea]
    v_yinn = v[:, inn]
    us_ = u_yo.reshape(512, 1024, 2).sum(-1)
    vs_ = v_yinn.reshape(512, 1024, 2).sum(-1)
    out = us_ + vs_
    return out

@@ -1,0 +1,222 @@
+from contextlib import ExitStack
+
+import concourse.mybir as mybir
+from concourse.masks import make_identity
+
+M, D, NODES, EDGES = 512, 512, 1024, 2048
+FLOPS = 2 * 2 * M * D * EDGES
+
+F32 = mybir.dt.float32
+BF16 = mybir.dt.bfloat16
+U32 = mybir.dt.uint32
+U16 = mybir.dt.uint16
+U8 = mybir.dt.uint8
+E4M3 = mybir.dt.float8_e4m3fn_x4
+E5M2 = mybir.dt.float8_e5m2_x4
+ACT = mybir.ActivationFunctionType
+ALU = mybir.AluOpType
+
+P = 128
+PACK = 4
+CHUNK = 512
+HALF = 1024
+GROUP = 16
+
+
+def tile_attend_gedge_sig_kernel(tc, dyT, hE, ws, wtt, dstoffs, innoffs, leaoffs, out):
+    nc = tc.nc
+    with ExitStack() as ctx:
+        lists = ctx.enter_context(tc.tile_pool(name="lists", bufs=1))
+        sb = ctx.enter_context(tc.tile_pool(name="sb", bufs=1))
+        ps = ctx.enter_context(tc.psum_pool(name="ps", bufs=1))
+
+        dst = lists.tile([P, EDGES // GROUP], U16, name="dst")
+        inn = lists.tile([P, EDGES // GROUP], U16, name="inn")
+        lea = lists.tile([P, EDGES // GROUP], U16, name="lea")
+
+        dy = [sb.tile([P, NODES], F32, name="dy%d" % t) for t in range(PACK)]
+        slope01 = [sb.tile([P, HALF], F32, name="slope01_%d" % t) for t in range(PACK)]
+        slope2 = sb.tile([P, PACK * CHUNK], F32, name="slope2")
+        slope3 = sb.tile([P, PACK * CHUNK], F32, name="slope3")
+        shared = sb.tile([P, 3 * HALF], F32, name="shared", align_bytes=64)
+        dz = [sb.tile([P, PACK * CHUNK], F32, name="dz%d" % k) for k in range(4)]
+        dzb3 = sb.tile([P, PACK * CHUNK], BF16, name="dzb3", align_bytes=64)
+        dz_codes = sb.tile([P, EDGES], U32, name="dz_codes", align_bytes=64)
+        dz_scales = sb.tile([P, EDGES], U8, name="dz_scales", align_bytes=64)
+        w_raw = [sb.tile([P, PACK, D], F32, name="w_raw%d" % a) for a in range(2)]
+        w_first = sb.tile([P, PACK * P], BF16, name="w_first", align_bytes=64)
+        w_codes = [sb.tile([P, D], U32, name="w_codes%d" % a, align_bytes=64) for a in range(2)]
+        w_scales = [sb.tile([P, D], U8, name="w_scales%d" % a, align_bytes=64) for a in range(2)]
+        uv = [[sb.tile([P, EDGES], F32, name="uv%d_%d" % (a, j)) for j in range(4)] for a in range(2)]
+        turned = [sb.tile([P, CHUNK], F32, name="turned%d" % h) for h in range(2)]
+        result = [sb.tile([P, CHUNK], F32, name="result%d" % h) for h in range(4)]
+        ident = sb.tile([P, P], F32, name="ident")
+        banks = [ps.tile([P, CHUNK], F32, name="bank%d" % b) for b in range(8)]
+
+        shared_bf = shared[:].bitcast(BF16)
+        dzb = [shared_bf[:, k * 2048 : (k + 1) * 2048] for k in range(3)] + [dzb3[:]]
+        h3 = shared[:].rearrange("p (t c) -> p t c", t=PACK)[:, :, 0:CHUNK]
+
+        dy_rows = dyT.rearrange("(p t) x -> p t x", t=PACK)
+        h_rows = hE.rearrange("(p t) c -> p t c", t=PACK)
+
+        nc.sync.dma_start(dst[:], dstoffs)
+        nc.sync.dma_start(slope01[0][:, 0:CHUNK], h_rows[:, 0, 0:CHUNK])
+        nc.sync.dma_start(dy[0][:], dy_rows[:, 0, :])
+        nc.sync.dma_start(slope01[0][:, CHUNK:HALF], h_rows[:, 0, CHUNK:HALF])
+        for t in range(1, PACK):
+            nc.sync.dma_start(slope01[t][:], h_rows[:, t, 0:HALF])
+            nc.sync.dma_start(dy[t][:], dy_rows[:, t, :])
+        s2 = slope2[:].rearrange("p (t c) -> p t c", t=PACK)
+        for t0 in (0, 2):
+            nc.sync.dma_start(s2[:, t0 : t0 + 2, :], h_rows[:, t0 : t0 + 2, 2 * CHUNK : 3 * CHUNK])
+        nc.sync.dma_start(h3, h_rows[:, :, 3 * CHUNK : 4 * CHUNK])
+        for a, w in enumerate((ws, wtt)):
+            nc.sync.dma_start(w_raw[a][:], w.rearrange("(p t) d -> p t d", t=PACK))
+        nc.sync.dma_start(lea[:], leaoffs)
+        nc.sync.dma_start(inn[:], innoffs)
+
+        make_identity(nc, ident[:])
+
+        def square(dest, h):
+            nc.scalar.activation(dest, h, ACT.Square, bias=-0.5, scale=1.0)
+
+        def slope_on_scalar(s):
+            nc.scalar.activation(s, s, ACT.Identity, bias=0.25, scale=-1.0)
+
+        def slope_on_vector(s):
+            nc.vector.tensor_scalar(s, s, -1.0, 0.25, ALU.mult, ALU.add)
+
+        def entries(offs, first, count):
+            return offs[:, first // GROUP : (first + count) // GROUP]
+
+        def gather_dz(k, t, s):
+            nc.vector.tensor_tensor(
+                dz[k][:, t * CHUNK : (t + 1) * CHUNK], dy[t][:].indirect(entries(dst, k * CHUNK, CHUNK)), s, ALU.mult
+            )
+
+        def interleave(copy, dest, planes):
+            copy(dest.rearrange("p (c i t) -> p c t i", i=4, t=PACK), planes.rearrange("p t (c i) -> p c t i", i=4))
+
+        def interleave_dz(copy, k):
+            interleave(copy, dzb[k], dz[k][:].rearrange("p (t c) -> p t c", t=PACK))
+
+        def quantise_dz(k):
+            cols = slice(k * CHUNK, (k + 1) * CHUNK)
+            nc.vector.quantize_mx(out=dz_codes[:, cols].bitcast(E5M2), scales=dz_scales[:, cols], in_=dzb[k])
+
+        def quantise_w(copy, a, d0, d1, stage):
+            interleave(copy, stage, w_raw[a][:, :, d0:d1])
+            return lambda: nc.vector.quantize_mx(
+                out=w_codes[a][:, d0:d1].bitcast(E4M3), scales=w_scales[a][:, d0:d1], in_=stage
+            )
+
+        def product(a, j, k, bank0):
+            bank = banks[bank0 + k]
+            wc = slice(j * P, (j + 1) * P)
+            cols = slice(k * CHUNK, (k + 1) * CHUNK)
+            nc.tensor.matmul_mx(
+                out=bank[:],
+                lhsT=w_codes[a][:, wc].bitcast(E4M3),
+                lhsT_scale=w_scales[a][:, wc],
+                rhs=dz_codes[:, cols].bitcast(E5M2),
+                rhs_scale=dz_scales[:, cols],
+                start=True,
+                stop=True,
+            )
+            nc.scalar.copy(uv[a][j][:, cols], bank[:])
+
+        for t in range(PACK):
+            parts = ((0, CHUNK), (CHUNK, HALF)) if t == 0 else ((0, HALF),)
+            for c0, c1 in parts:
+                square(slope01[t][:, c0:c1], slope01[t][:, c0:c1])
+                slope_on_scalar(slope01[t][:, c0:c1])
+            for k in range(2):
+                gather_dz(k, t, slope01[t][:, k * CHUNK : (k + 1) * CHUNK])
+        for t in range(PACK):
+            s = slope2[:, t * CHUNK : (t + 1) * CHUNK]
+            square(s, s)
+            slope_on_scalar(s)
+            gather_dz(2, t, s)
+        for t in range(PACK):
+            square(slope3[:, t * CHUNK : (t + 1) * CHUNK], h3[:, t, :])
+        for t0 in (0, 2):
+            slope_on_vector(slope3[:, t0 * CHUNK : (t0 + 2) * CHUNK])
+        for t in range(PACK):
+            gather_dz(3, t, slope3[:, t * CHUNK : (t + 1) * CHUNK])
+        q_first = quantise_w(nc.vector.tensor_copy, 0, 0, P, w_first[:])
+        interleave_dz(nc.vector.tensor_copy, 3)
+        q_first()
+        quantise_dz(3)
+        for k in range(3):
+            interleave_dz(nc.scalar.copy, k)
+            quantise_dz(k)
+        for k in (3, 0, 1, 2):
+            product(0, 0, k, 0)
+
+        late = dzb[2]
+        q_a = quantise_w(nc.vector.tensor_copy, 1, 0, 2 * P, late[:, 0:1024])
+        q_b = quantise_w(nc.vector.tensor_copy, 0, P, 2 * P, late[:, 1024:1536])
+        q_a()
+        q_b()
+        for a, j in ((1, 0), (0, 1), (1, 1)):
+            for k in range(4):
+                product(a, j, k, 4 * a)
+
+        def gather_half(j, h):
+            from_u = slope01[(2 * j + h) % PACK]
+            both = dz[j][:, h * HALF : (h + 1) * HALF]
+            nc.vector.tensor_copy(from_u[:], uv[0][j][:].indirect(entries(lea, h * HALF, HALF)))
+            nc.vector.tensor_tensor(both, uv[1][j][:].indirect(entries(inn, h * HALF, HALF)), from_u[:], ALU.add)
+
+        def store(j, h, res):
+            nc.sync.dma_start(out[j * P : (j + 1) * P, h * CHUNK : (h + 1) * CHUNK], res[:])
+
+        def pair_sums_on_tensor(j, parts):
+            for n, (b0, nb) in enumerate(parts):
+                for b in range(nb):
+                    for e in range(2):
+                        c0 = (b0 + b) * 2 * P
+                        nc.tensor.matmul(
+                            banks[6 + n][:, b * P : (b + 1) * P],
+                            dz[j][:, c0 + e : c0 + 2 * P : 2],
+                            ident[:],
+                            start=(e == 0),
+                            stop=(e == 1),
+                            is_transpose=True,
+                        )
+                nc.scalar.copy(turned[n][:, 0 : nb * P], banks[6 + n][:, 0 : nb * P])
+            for n, (b0, nb) in enumerate(parts):
+                res = result[(2 * j + n) % 4]
+                for b in range(nb):
+                    nc.tensor.transpose(banks[4 + n][:, b * P : (b + 1) * P], turned[n][:, b * P : (b + 1) * P], ident[:])
+                nc.scalar.copy(res[:, 0 : nb * P], banks[4 + n][:, 0 : nb * P])
+                nc.sync.dma_start(out[j * P : (j + 1) * P, b0 * P : (b0 + nb) * P], res[:, 0 : nb * P])
+
+        def products(a, j, bank0):
+            for k in range(4):
+                product(a, j, k, bank0)
+
+        halves = ((0, 4), (4, 4))
+        gather_half(0, 0)
+        gather_half(0, 1)
+        q_c = quantise_w(nc.scalar.copy, 0, 2 * P, D, late[:, 0:1024])
+        q_d = quantise_w(nc.scalar.copy, 1, 2 * P, D, late[:, 1024:2048])
+        gather_half(1, 0)
+        q_c()
+        q_d()
+        gather_half(1, 1)
+        pair_sums_on_tensor(0, halves)
+        products(0, 2, 4)
+        products(1, 2, 0)
+        products(0, 3, 0)
+        products(1, 3, 0)
+        pair_sums_on_tensor(1, halves)
+        gather_half(2, 0)
+        gather_half(2, 1)
+        pair_sums_on_tensor(2, halves)
+        gather_half(3, 0)
+        pair_sums_on_tensor(3, ((0, 2), (2, 2)))
+        gather_half(3, 1)
+        nc.vector.tensor_tensor(result[0][:], dz[3][:, HALF : EDGES : 2], dz[3][:, HALF + 1 : EDGES : 2], ALU.add)
+        store(3, 1, result[0])

@@ -17,10 +17,16 @@ ACT = mybir.ActivationFunctionType
 ALU = mybir.AluOpType
 
 P = 128
-PACK = 4
+PLANES = 4
 CHUNK = 512
-HALF = 1024
-GROUP = 16
+CHUNKS = EDGES // CHUNK
+LAST_CHUNK = CHUNKS - 1
+ROW_TILES = D // P
+LAST_TILE = ROW_TILES - 1
+HALF = EDGES // 2
+PER_COLUMN = 16
+RUN = 4
+U, V = 0, 1
 
 
 def tile_attend_gedge_sig_kernel(tc, dyT, hE, ws, wtt, dstoffs, innoffs, leaoffs, out):
@@ -30,193 +36,212 @@ def tile_attend_gedge_sig_kernel(tc, dyT, hE, ws, wtt, dstoffs, innoffs, leaoffs
         sb = ctx.enter_context(tc.tile_pool(name="sb", bufs=1))
         ps = ctx.enter_context(tc.psum_pool(name="ps", bufs=1))
 
-        dst = lists.tile([P, EDGES // GROUP], U16, name="dst")
-        inn = lists.tile([P, EDGES // GROUP], U16, name="inn")
-        lea = lists.tile([P, EDGES // GROUP], U16, name="lea")
+        dst = lists.tile([P, EDGES // PER_COLUMN], U16, name="dst")
+        inn = lists.tile([P, EDGES // PER_COLUMN], U16, name="inn")
+        lea = lists.tile([P, EDGES // PER_COLUMN], U16, name="lea")
 
-        dy = [sb.tile([P, NODES], F32, name="dy%d" % t) for t in range(PACK)]
-        slope01 = [sb.tile([P, HALF], F32, name="slope01_%d" % t) for t in range(PACK)]
-        slope2 = sb.tile([P, PACK * CHUNK], F32, name="slope2")
-        slope3 = sb.tile([P, PACK * CHUNK], F32, name="slope3")
-        shared = sb.tile([P, 3 * HALF], F32, name="shared", align_bytes=64)
-        dz = [sb.tile([P, PACK * CHUNK], F32, name="dz%d" % k) for k in range(4)]
-        dzb3 = sb.tile([P, PACK * CHUNK], BF16, name="dzb3", align_bytes=64)
+        dy = [sb.tile([P, NODES], F32, name="dy%d" % t) for t in range(PLANES)]
+        early = [sb.tile([P, LAST_CHUNK * CHUNK], F32, name="early%d" % t) for t in range(PLANES)]
+        last = sb.tile([P, PLANES * CHUNK], F32, name="last")
+        shared = sb.tile([P, LAST_CHUNK * PLANES * CHUNK // 2], F32, name="shared", align_bytes=64)
+        wide = [sb.tile([P, PLANES * CHUNK], F32, name="wide%d" % k) for k in range(CHUNKS)]
+        dz_last = sb.tile([P, PLANES * CHUNK], BF16, name="dz_last", align_bytes=64)
         dz_codes = sb.tile([P, EDGES], U32, name="dz_codes", align_bytes=64)
         dz_scales = sb.tile([P, EDGES], U8, name="dz_scales", align_bytes=64)
-        w_raw = [sb.tile([P, PACK, D], F32, name="w_raw%d" % a) for a in range(2)]
-        w_first = sb.tile([P, PACK * P], BF16, name="w_first", align_bytes=64)
-        w_codes = [sb.tile([P, D], U32, name="w_codes%d" % a, align_bytes=64) for a in range(2)]
-        w_scales = [sb.tile([P, D], U8, name="w_scales%d" % a, align_bytes=64) for a in range(2)]
-        uv = [[sb.tile([P, EDGES], F32, name="uv%d_%d" % (a, j)) for j in range(4)] for a in range(2)]
-        turned = [sb.tile([P, CHUNK], F32, name="turned%d" % h) for h in range(2)]
-        result = [sb.tile([P, CHUNK], F32, name="result%d" % h) for h in range(4)]
+        w_raw = [sb.tile([P, PLANES, D], F32, name="w_raw%d" % a) for a in (U, V)]
+        w_first = sb.tile([P, PLANES * P], BF16, name="w_first", align_bytes=64)
+        w_codes = [sb.tile([P, D], U32, name="w_codes%d" % a, align_bytes=64) for a in (U, V)]
+        w_scales = [sb.tile([P, D], U8, name="w_scales%d" % a, align_bytes=64) for a in (U, V)]
+        uv = [[sb.tile([P, EDGES], F32, name="uv%d_%d" % (a, j)) for j in range(ROW_TILES)] for a in (U, V)]
+        turned = [sb.tile([P, CHUNK], F32, name="turned%d" % n) for n in range(2)]
+        result = [sb.tile([P, CHUNK], F32, name="result%d" % n) for n in range(4)]
+        tail = sb.tile([P, NODES], F32, name="tail")
         ident = sb.tile([P, P], F32, name="ident")
-        banks = [ps.tile([P, CHUNK], F32, name="bank%d" % b) for b in range(8)]
+        banks = [ps.tile([P, CHUNK], F32, name="bank%d" % b) for b in range(2 * CHUNKS)]
 
         shared_bf = shared[:].bitcast(BF16)
-        dzb = [shared_bf[:, k * 2048 : (k + 1) * 2048] for k in range(3)] + [dzb3[:]]
-        h3 = shared[:].rearrange("p (t c) -> p t c", t=PACK)[:, :, 0:CHUNK]
+        dz_bf = [shared_bf[:, k * PLANES * CHUNK : (k + 1) * PLANES * CHUNK] for k in range(LAST_CHUNK)]
+        dz_bf.append(dz_last[:])
 
-        dy_rows = dyT.rearrange("(p t) x -> p t x", t=PACK)
-        h_rows = hE.rearrange("(p t) c -> p t c", t=PACK)
+        dy_planes = dyT.rearrange("(p t) x -> p t x", t=PLANES)
+        h_planes = hE.rearrange("(p t) c -> p t c", t=PLANES)
 
-        nc.sync.dma_start(dst[:], dstoffs)
-        nc.sync.dma_start(slope01[0][:, 0:CHUNK], h_rows[:, 0, 0:CHUNK])
-        nc.sync.dma_start(dy[0][:], dy_rows[:, 0, :])
-        nc.sync.dma_start(slope01[0][:, CHUNK:HALF], h_rows[:, 0, CHUNK:HALF])
-        for t in range(1, PACK):
-            nc.sync.dma_start(slope01[t][:], h_rows[:, t, 0:HALF])
-            nc.sync.dma_start(dy[t][:], dy_rows[:, t, :])
-        s2 = slope2[:].rearrange("p (t c) -> p t c", t=PACK)
-        for t0 in (0, 2):
-            nc.sync.dma_start(s2[:, t0 : t0 + 2, :], h_rows[:, t0 : t0 + 2, 2 * CHUNK : 3 * CHUNK])
-        nc.sync.dma_start(h3, h_rows[:, :, 3 * CHUNK : 4 * CHUNK])
-        for a, w in enumerate((ws, wtt)):
-            nc.sync.dma_start(w_raw[a][:], w.rearrange("(p t) d -> p t d", t=PACK))
+        def load_h(t, k0, k1):
+            nc.sync.dma_start(early[t][:, k0 * CHUNK : k1 * CHUNK], h_planes[:, t, k0 * CHUNK : k1 * CHUNK])
+
+        for t in range(PLANES):
+            if t == 0:
+                load_h(t, 0, 1)
+                load_h(t, 1, 2)
+                nc.sync.dma_start(dst[:], dstoffs)
+            else:
+                load_h(t, 0, 2)
+            nc.sync.dma_start(dy[t][:], dy_planes[:, t, :])
+            load_h(t, 2, LAST_CHUNK)
+        nc.sync.dma_start(last[:].rearrange("p (t c) -> p t c", t=PLANES), h_planes[:, :, LAST_CHUNK * CHUNK :])
+        for a, w in ((U, ws), (V, wtt)):
+            nc.sync.dma_start(w_raw[a][:], w.rearrange("(p t) d -> p t d", t=PLANES))
         nc.sync.dma_start(lea[:], leaoffs)
         nc.sync.dma_start(inn[:], innoffs)
 
         make_identity(nc, ident[:])
 
+        def entries(offsets, first, count):
+            return offsets[:, first // PER_COLUMN : (first + count) // PER_COLUMN]
+
         def square(dest, h):
             nc.scalar.activation(dest, h, ACT.Square, bias=-0.5, scale=1.0)
 
-        def slope_on_scalar(s):
-            nc.scalar.activation(s, s, ACT.Identity, bias=0.25, scale=-1.0)
+        def quarter_less(dest, squares):
+            nc.scalar.activation(dest, squares, ACT.Identity, bias=0.25, scale=-1.0)
 
-        def slope_on_vector(s):
-            nc.vector.tensor_scalar(s, s, -1.0, 0.25, ALU.mult, ALU.add)
-
-        def entries(offs, first, count):
-            return offs[:, first // GROUP : (first + count) // GROUP]
-
-        def gather_dz(k, t, s):
-            nc.vector.tensor_tensor(
-                dz[k][:, t * CHUNK : (t + 1) * CHUNK], dy[t][:].indirect(entries(dst, k * CHUNK, CHUNK)), s, ALU.mult
-            )
+        def gather_dz(k, t, slope):
+            picked = dy[t][:].indirect(entries(dst, k * CHUNK, CHUNK))
+            nc.vector.tensor_tensor(wide[k][:, t * CHUNK : (t + 1) * CHUNK], picked, slope, ALU.mult)
 
         def interleave(copy, dest, planes):
-            copy(dest.rearrange("p (c i t) -> p c t i", i=4, t=PACK), planes.rearrange("p t (c i) -> p c t i", i=4))
+            copy(
+                dest.rearrange("p (c i t) -> p c t i", i=RUN, t=PLANES),
+                planes.rearrange("p t (c i) -> p c t i", i=RUN),
+            )
 
         def interleave_dz(copy, k):
-            interleave(copy, dzb[k], dz[k][:].rearrange("p (t c) -> p t c", t=PACK))
+            interleave(copy, dz_bf[k], wide[k][:].rearrange("p (t c) -> p t c", t=PLANES))
 
         def quantise_dz(k):
             cols = slice(k * CHUNK, (k + 1) * CHUNK)
-            nc.vector.quantize_mx(out=dz_codes[:, cols].bitcast(E5M2), scales=dz_scales[:, cols], in_=dzb[k])
+            nc.vector.quantize_mx(out=dz_codes[:, cols].bitcast(E5M2), scales=dz_scales[:, cols], in_=dz_bf[k])
 
-        def quantise_w(copy, a, d0, d1, stage):
-            interleave(copy, stage, w_raw[a][:, :, d0:d1])
-            return lambda: nc.vector.quantize_mx(
-                out=w_codes[a][:, d0:d1].bitcast(E4M3), scales=w_scales[a][:, d0:d1], in_=stage
-            )
+        def interleave_w(copy, a, j0, j1, stage):
+            interleave(copy, stage, w_raw[a][:, :, j0 * P : j1 * P])
 
-        def product(a, j, k, bank0):
-            bank = banks[bank0 + k]
-            wc = slice(j * P, (j + 1) * P)
-            cols = slice(k * CHUNK, (k + 1) * CHUNK)
-            nc.tensor.matmul_mx(
-                out=bank[:],
-                lhsT=w_codes[a][:, wc].bitcast(E4M3),
-                lhsT_scale=w_scales[a][:, wc],
-                rhs=dz_codes[:, cols].bitcast(E5M2),
-                rhs_scale=dz_scales[:, cols],
-                start=True,
-                stop=True,
-            )
-            nc.scalar.copy(uv[a][j][:, cols], bank[:])
+        def quantise_w(a, j0, j1, stage):
+            cols = slice(j0 * P, j1 * P)
+            nc.vector.quantize_mx(out=w_codes[a][:, cols].bitcast(E4M3), scales=w_scales[a][:, cols], in_=stage)
 
-        for t in range(PACK):
-            parts = ((0, CHUNK), (CHUNK, HALF)) if t == 0 else ((0, HALF),)
-            for c0, c1 in parts:
-                square(slope01[t][:, c0:c1], slope01[t][:, c0:c1])
-                slope_on_scalar(slope01[t][:, c0:c1])
-            for k in range(2):
-                gather_dz(k, t, slope01[t][:, k * CHUNK : (k + 1) * CHUNK])
-        for t in range(PACK):
-            s = slope2[:, t * CHUNK : (t + 1) * CHUNK]
-            square(s, s)
-            slope_on_scalar(s)
-            gather_dz(2, t, s)
-        for t in range(PACK):
-            square(slope3[:, t * CHUNK : (t + 1) * CHUNK], h3[:, t, :])
-        for t0 in (0, 2):
-            slope_on_vector(slope3[:, t0 * CHUNK : (t0 + 2) * CHUNK])
-        for t in range(PACK):
-            gather_dz(3, t, slope3[:, t * CHUNK : (t + 1) * CHUNK])
-        q_first = quantise_w(nc.vector.tensor_copy, 0, 0, P, w_first[:])
-        interleave_dz(nc.vector.tensor_copy, 3)
-        q_first()
-        quantise_dz(3)
-        for k in range(3):
+        def products(a, j, chunks):
+            rows = slice(j * P, (j + 1) * P)
+            for k in chunks:
+                cols = slice(k * CHUNK, (k + 1) * CHUNK)
+                bank = banks[CHUNKS * a + k]
+                nc.tensor.matmul_mx(
+                    out=bank[:],
+                    lhsT=w_codes[a][:, rows].bitcast(E4M3),
+                    lhsT_scale=w_scales[a][:, rows],
+                    rhs=dz_codes[:, cols].bitcast(E5M2),
+                    rhs_scale=dz_scales[:, cols],
+                    start=True,
+                    stop=True,
+                )
+                nc.scalar.copy(uv[a][j][:, cols], bank[:])
+
+        ahead = early[0][:, 0 : 2 * CHUNK]
+        for k in range(2):
+            square(ahead[:, k * CHUNK : (k + 1) * CHUNK], ahead[:, k * CHUNK : (k + 1) * CHUNK])
+        nc.vector.tensor_scalar(ahead, ahead, -1.0, 0.25, ALU.mult, ALU.add)
+        for t in range(PLANES):
+            for k in range(LAST_CHUNK):
+                slope = early[t][:, k * CHUNK : (k + 1) * CHUNK]
+                if t > 0 or k >= 2:
+                    square(slope, slope)
+                    quarter_less(slope, slope)
+                gather_dz(k, t, slope)
+
+        squares = shared[:].rearrange("p (r c) -> p r c", r=CHUNK // P)
+        for t in range(PLANES):
+            slope = last[:, t * CHUNK : (t + 1) * CHUNK]
+            in_runs = slope.rearrange("p (r c) -> p r c", c=P)
+            square(squares[:, :, t * P : (t + 1) * P], in_runs)
+            quarter_less(in_runs, squares[:, :, t * P : (t + 1) * P])
+            gather_dz(LAST_CHUNK, t, slope)
+
+        interleave_w(nc.vector.tensor_copy, U, 0, 1, w_first[:])
+        interleave_dz(nc.vector.tensor_copy, LAST_CHUNK)
+        quantise_w(U, 0, 1, w_first[:])
+        quantise_dz(LAST_CHUNK)
+        for k in range(LAST_CHUNK):
             interleave_dz(nc.scalar.copy, k)
             quantise_dz(k)
-        for k in (3, 0, 1, 2):
-            product(0, 0, k, 0)
+        products(U, 0, [LAST_CHUNK] + list(range(LAST_CHUNK)))
 
-        late = dzb[2]
-        q_a = quantise_w(nc.vector.tensor_copy, 1, 0, 2 * P, late[:, 0:1024])
-        q_b = quantise_w(nc.vector.tensor_copy, 0, P, 2 * P, late[:, 1024:1536])
-        q_a()
-        q_b()
-        for a, j in ((1, 0), (0, 1), (1, 1)):
-            for k in range(4):
-                product(a, j, k, 4 * a)
+        stage = dz_bf[LAST_CHUNK - 1]
+        stage_a, stage_b = stage[:, 0 : 2 * PLANES * P], stage[:, 2 * PLANES * P :]
+        interleave_w(nc.vector.tensor_copy, V, 0, 2, stage_a)
+        interleave_w(nc.vector.tensor_copy, U, 1, 2, stage_b[:, 0 : PLANES * P])
+        quantise_w(V, 0, 2, stage_a)
+        quantise_w(U, 1, 2, stage_b[:, 0 : PLANES * P])
+        products(V, 0, range(CHUNKS))
+        products(U, 1, range(CHUNKS))
+        interleave_w(nc.scalar.copy, U, 2, ROW_TILES, stage_a)
+        interleave_w(nc.scalar.copy, V, 2, ROW_TILES, stage_b)
+        products(V, 1, range(CHUNKS))
 
-        def gather_half(j, h):
-            from_u = slope01[(2 * j + h) % PACK]
-            both = dz[j][:, h * HALF : (h + 1) * HALF]
-            nc.vector.tensor_copy(from_u[:], uv[0][j][:].indirect(entries(lea, h * HALF, HALF)))
-            nc.vector.tensor_tensor(both, uv[1][j][:].indirect(entries(inn, h * HALF, HALF)), from_u[:], ALU.add)
+        def gather_u(j, first, count, dest):
+            nc.vector.tensor_copy(dest, uv[U][j][:].indirect(entries(lea, first, count)))
 
-        def store(j, h, res):
-            nc.sync.dma_start(out[j * P : (j + 1) * P, h * CHUNK : (h + 1) * CHUNK], res[:])
+        def gather_v(j, first, count, from_u):
+            picked = uv[V][j][:].indirect(entries(inn, first, count))
+            nc.vector.tensor_tensor(wide[j][:, first : first + count], picked, from_u, ALU.add)
 
-        def pair_sums_on_tensor(j, parts):
-            for n, (b0, nb) in enumerate(parts):
-                for b in range(nb):
-                    for e in range(2):
-                        c0 = (b0 + b) * 2 * P
+        def gather_half(j, h, from_u):
+            gather_u(j, h * HALF, HALF, from_u)
+            gather_v(j, h * HALF, HALF, from_u)
+
+        def ring(j, h):
+            return early[(2 * j + h) % PLANES][:, 0:HALF]
+
+        def pair_sums_on_tensor(j, blocks):
+            width = blocks * P
+            for n in range(2):
+                for b in range(blocks):
+                    first = (n * blocks + b) * 2 * P
+                    for odd in range(2):
                         nc.tensor.matmul(
                             banks[6 + n][:, b * P : (b + 1) * P],
-                            dz[j][:, c0 + e : c0 + 2 * P : 2],
+                            wide[j][:, first + odd : first + 2 * P : 2],
                             ident[:],
-                            start=(e == 0),
-                            stop=(e == 1),
+                            start=(odd == 0),
+                            stop=(odd == 1),
                             is_transpose=True,
                         )
-                nc.scalar.copy(turned[n][:, 0 : nb * P], banks[6 + n][:, 0 : nb * P])
-            for n, (b0, nb) in enumerate(parts):
-                res = result[(2 * j + n) % 4]
-                for b in range(nb):
-                    nc.tensor.transpose(banks[4 + n][:, b * P : (b + 1) * P], turned[n][:, b * P : (b + 1) * P], ident[:])
-                nc.scalar.copy(res[:, 0 : nb * P], banks[4 + n][:, 0 : nb * P])
-                nc.sync.dma_start(out[j * P : (j + 1) * P, b0 * P : (b0 + nb) * P], res[:, 0 : nb * P])
+                nc.scalar.copy(turned[n][:, 0:width], banks[6 + n][:, 0:width])
+            for n in range(2):
+                sums = result[(2 * j + n) % 4][:, 0:width]
+                for b in range(blocks):
+                    cols = slice(b * P, (b + 1) * P)
+                    nc.tensor.transpose(banks[4 + n][:, cols], turned[n][:, cols], ident[:])
+                nc.scalar.copy(sums, banks[4 + n][:, 0:width])
+                nc.sync.dma_start(out[j * P : (j + 1) * P, n * width : (n + 1) * width], sums)
 
-        def products(a, j, bank0):
-            for k in range(4):
-                product(a, j, k, bank0)
+        whole = NODES // (2 * P)
+        for h in range(2):
+            gather_half(0, h, ring(0, h))
+        quantise_w(U, 2, ROW_TILES, stage_a)
+        quantise_w(V, 2, ROW_TILES, stage_b)
+        gather_half(1, 0, stage.bitcast(F32))
+        gather_half(1, 1, ring(1, 1))
+        for j in (0, 1):
+            pair_sums_on_tensor(j, whole)
+            products(U, j + 2, range(CHUNKS))
+            products(V, j + 2, range(CHUNKS))
+        for h in range(2):
+            gather_half(2, h, ring(2, h))
+        pair_sums_on_tensor(2, whole)
 
-        halves = ((0, 4), (4, 4))
-        gather_half(0, 0)
-        gather_half(0, 1)
-        q_c = quantise_w(nc.scalar.copy, 0, 2 * P, D, late[:, 0:1024])
-        q_d = quantise_w(nc.scalar.copy, 1, 2 * P, D, late[:, 1024:2048])
-        gather_half(1, 0)
-        q_c()
-        q_d()
-        gather_half(1, 1)
-        pair_sums_on_tensor(0, halves)
-        products(0, 2, 4)
-        products(1, 2, 0)
-        products(0, 3, 0)
-        products(1, 3, 0)
-        pair_sums_on_tensor(1, halves)
-        gather_half(2, 0)
-        gather_half(2, 1)
-        pair_sums_on_tensor(2, halves)
-        gather_half(3, 0)
-        pair_sums_on_tensor(3, ((0, 2), (2, 2)))
-        gather_half(3, 1)
-        nc.vector.tensor_tensor(result[0][:], dz[3][:, HALF : EDGES : 2], dz[3][:, HALF + 1 : EDGES : 2], ALU.add)
-        store(3, 1, result[0])
+        for h in range(2):
+            gather_u(LAST_TILE, h * HALF, HALF, last[:, h * HALF : (h + 1) * HALF])
+        quarter = EDGES // 4
+
+        def pair_sums_on_vector(q):
+            both = wide[LAST_TILE][:, q * quarter : (q + 1) * quarter]
+            nodes = slice(q * quarter // 2, (q + 1) * quarter // 2)
+            nc.vector.tensor_tensor(tail[:, nodes], both[:, 0::2], both[:, 1::2], ALU.add)
+            nc.sync.dma_start(out[LAST_TILE * P :, nodes], tail[:, nodes])
+
+        for q in range(4):
+            gather_v(LAST_TILE, q * quarter, quarter, last[:, q * quarter : (q + 1) * quarter])
+            if q == 0:
+                pair_sums_on_tensor(LAST_TILE, 1)
+            if q >= 2:
+                pair_sums_on_vector(q - 1)
+        pair_sums_on_vector(3)

@@ -184,8 +184,10 @@ def tile_attend_gedge_sig_kernel(tc, dyT, hE, ws, wtt, dstoffs, innoffs, leaoffs
             nc.vector.tensor_tensor(wide[j][:, first : first + count], picked, from_u, ALU.add)
 
         def gather_half(j, h, from_u):
+            both = wide[j][:, h * HALF : (h + 1) * HALF]
             gather_u(j, h * HALF, HALF, from_u)
-            gather_v(j, h * HALF, HALF, from_u)
+            nc.vector.tensor_copy(both, uv[V][j][:].indirect(entries(inn, h * HALF, HALF)))
+            nc.gpsimd.tensor_tensor(both, both, from_u, ALU.add)
 
         def ring(j, h):
             return early[(2 * j + h) % PLANES][:, 0:HALF]

from contextlib import ExitStack

import concourse.mybir as mybir
from concourse.masks import make_identity

M, D, NODES, EDGES = 512, 512, 1024, 2048
FLOPS = 2 * 2 * M * D * EDGES

F32 = mybir.dt.float32
BF16 = mybir.dt.bfloat16
U32 = mybir.dt.uint32
U16 = mybir.dt.uint16
U8 = mybir.dt.uint8
E4M3 = mybir.dt.float8_e4m3fn_x4
E5M2 = mybir.dt.float8_e5m2_x4
ACT = mybir.ActivationFunctionType
ALU = mybir.AluOpType

P = 128
PLANES = 4
CHUNK = 512
CHUNKS = EDGES // CHUNK
LAST_CHUNK = CHUNKS - 1
ROW_TILES = D // P
LAST_TILE = ROW_TILES - 1
HALF = EDGES // 2
PER_COLUMN = 16
RUN = 4
U, V = 0, 1


def tile_attend_gedge_sig_kernel(tc, dyT, hE, ws, wtt, dstoffs, innoffs, leaoffs, out):
    nc = tc.nc
    with ExitStack() as ctx:
        lists = ctx.enter_context(tc.tile_pool(name="lists", bufs=1))
        sb = ctx.enter_context(tc.tile_pool(name="sb", bufs=1))
        ps = ctx.enter_context(tc.psum_pool(name="ps", bufs=1))

        dst = lists.tile([P, EDGES // PER_COLUMN], U16, name="dst")
        inn = lists.tile([P, EDGES // PER_COLUMN], U16, name="inn")
        lea = lists.tile([P, EDGES // PER_COLUMN], U16, name="lea")

        dy = [sb.tile([P, NODES], F32, name="dy%d" % t) for t in range(PLANES)]
        early = [sb.tile([P, LAST_CHUNK * CHUNK], F32, name="early%d" % t) for t in range(PLANES)]
        last = sb.tile([P, PLANES * CHUNK], F32, name="last")
        shared = sb.tile([P, LAST_CHUNK * PLANES * CHUNK // 2], F32, name="shared", align_bytes=64)
        wide = [sb.tile([P, PLANES * CHUNK], F32, name="wide%d" % k) for k in range(CHUNKS)]
        dz_last = sb.tile([P, PLANES * CHUNK], BF16, name="dz_last", align_bytes=64)
        dz_codes = sb.tile([P, EDGES], U32, name="dz_codes", align_bytes=64)
        dz_scales = sb.tile([P, EDGES], U8, name="dz_scales", align_bytes=64)
        w_raw = [sb.tile([P, PLANES, D], F32, name="w_raw%d" % a) for a in (U, V)]
        w_first = sb.tile([P, PLANES * P], BF16, name="w_first", align_bytes=64)
        w_codes = [sb.tile([P, D], U32, name="w_codes%d" % a, align_bytes=64) for a in (U, V)]
        w_scales = [sb.tile([P, D], U8, name="w_scales%d" % a, align_bytes=64) for a in (U, V)]
        uv = [[sb.tile([P, EDGES], F32, name="uv%d_%d" % (a, j)) for j in range(ROW_TILES)] for a in (U, V)]
        turned = [sb.tile([P, CHUNK], F32, name="turned%d" % n) for n in range(2)]
        result = [sb.tile([P, CHUNK], F32, name="result%d" % n) for n in range(4)]
        tail = sb.tile([P, NODES], F32, name="tail")
        ident = sb.tile([P, P], F32, name="ident")
        banks = [ps.tile([P, CHUNK], F32, name="bank%d" % b) for b in range(2 * CHUNKS)]

        shared_bf = shared[:].bitcast(BF16)
        dz_bf = [shared_bf[:, k * PLANES * CHUNK : (k + 1) * PLANES * CHUNK] for k in range(LAST_CHUNK)]
        dz_bf.append(dz_last[:])

        dy_planes = dyT.rearrange("(p t) x -> p t x", t=PLANES)
        h_planes = hE.rearrange("(p t) c -> p t c", t=PLANES)

        def load_h(t, k0, k1):
            nc.sync.dma_start(early[t][:, k0 * CHUNK : k1 * CHUNK], h_planes[:, t, k0 * CHUNK : k1 * CHUNK])

        for t in range(PLANES):
            if t == 0:
                load_h(t, 0, 1)
                load_h(t, 1, 2)
                nc.sync.dma_start(dst[:], dstoffs)
            else:
                load_h(t, 0, 2)
            nc.sync.dma_start(dy[t][:], dy_planes[:, t, :])
            load_h(t, 2, LAST_CHUNK)
        nc.sync.dma_start(last[:].rearrange("p (t c) -> p t c", t=PLANES), h_planes[:, :, LAST_CHUNK * CHUNK :])
        for a, w in ((U, ws), (V, wtt)):
            nc.sync.dma_start(w_raw[a][:], w.rearrange("(p t) d -> p t d", t=PLANES))
        nc.sync.dma_start(lea[:], leaoffs)
        nc.sync.dma_start(inn[:], innoffs)

        make_identity(nc, ident[:])

        def entries(offsets, first, count):
            return offsets[:, first // PER_COLUMN : (first + count) // PER_COLUMN]

        def square(dest, h):
            nc.scalar.activation(dest, h, ACT.Square, bias=-0.5, scale=1.0)

        def quarter_less(dest, squares):
            nc.scalar.activation(dest, squares, ACT.Identity, bias=0.25, scale=-1.0)

        def gather_dz(k, t, slope):
            picked = dy[t][:].indirect(entries(dst, k * CHUNK, CHUNK))
            nc.vector.tensor_tensor(wide[k][:, t * CHUNK : (t + 1) * CHUNK], picked, slope, ALU.mult)

        def interleave(copy, dest, planes):
            copy(
                dest.rearrange("p (c i t) -> p c t i", i=RUN, t=PLANES),
                planes.rearrange("p t (c i) -> p c t i", i=RUN),
            )

        def interleave_dz(copy, k):
            interleave(copy, dz_bf[k], wide[k][:].rearrange("p (t c) -> p t c", t=PLANES))

        def quantise_dz(k):
            cols = slice(k * CHUNK, (k + 1) * CHUNK)
            nc.vector.quantize_mx(out=dz_codes[:, cols].bitcast(E5M2), scales=dz_scales[:, cols], in_=dz_bf[k])

        def interleave_w(copy, a, j0, j1, stage):
            interleave(copy, stage, w_raw[a][:, :, j0 * P : j1 * P])

        def quantise_w(a, j0, j1, stage):
            cols = slice(j0 * P, j1 * P)
            nc.vector.quantize_mx(out=w_codes[a][:, cols].bitcast(E4M3), scales=w_scales[a][:, cols], in_=stage)

        def products(a, j, chunks):
            rows = slice(j * P, (j + 1) * P)
            for k in chunks:
                cols = slice(k * CHUNK, (k + 1) * CHUNK)
                bank = banks[CHUNKS * a + k]
                nc.tensor.matmul_mx(
                    out=bank[:],
                    lhsT=w_codes[a][:, rows].bitcast(E4M3),
                    lhsT_scale=w_scales[a][:, rows],
                    rhs=dz_codes[:, cols].bitcast(E5M2),
                    rhs_scale=dz_scales[:, cols],
                    start=True,
                    stop=True,
                )
                nc.scalar.copy(uv[a][j][:, cols], bank[:])

        ahead = early[0][:, 0 : 2 * CHUNK]
        for k in range(2):
            square(ahead[:, k * CHUNK : (k + 1) * CHUNK], ahead[:, k * CHUNK : (k + 1) * CHUNK])
        nc.vector.tensor_scalar(ahead, ahead, -1.0, 0.25, ALU.mult, ALU.add)
        for t in range(PLANES):
            for k in range(LAST_CHUNK):
                slope = early[t][:, k * CHUNK : (k + 1) * CHUNK]
                if t > 0 or k >= 2:
                    square(slope, slope)
                    quarter_less(slope, slope)
                gather_dz(k, t, slope)

        squares = shared[:].rearrange("p (r c) -> p r c", r=CHUNK // P)
        for t in range(PLANES):
            slope = last[:, t * CHUNK : (t + 1) * CHUNK]
            in_runs = slope.rearrange("p (r c) -> p r c", c=P)
            square(squares[:, :, t * P : (t + 1) * P], in_runs)
            quarter_less(in_runs, squares[:, :, t * P : (t + 1) * P])
            gather_dz(LAST_CHUNK, t, slope)

        interleave_w(nc.vector.tensor_copy, U, 0, 1, w_first[:])
        interleave_dz(nc.vector.tensor_copy, LAST_CHUNK)
        quantise_w(U, 0, 1, w_first[:])
        quantise_dz(LAST_CHUNK)
        for k in range(LAST_CHUNK):
            interleave_dz(nc.scalar.copy, k)
            quantise_dz(k)
        products(U, 0, [LAST_CHUNK] + list(range(LAST_CHUNK)))

        stage = dz_bf[LAST_CHUNK - 1]
        stage_a, stage_b = stage[:, 0 : 2 * PLANES * P], stage[:, 2 * PLANES * P :]
        interleave_w(nc.vector.tensor_copy, V, 0, 2, stage_a)
        interleave_w(nc.vector.tensor_copy, U, 1, 2, stage_b[:, 0 : PLANES * P])
        quantise_w(V, 0, 2, stage_a)
        quantise_w(U, 1, 2, stage_b[:, 0 : PLANES * P])
        products(V, 0, range(CHUNKS))
        products(U, 1, range(CHUNKS))
        interleave_w(nc.scalar.copy, U, 2, ROW_TILES, stage_a)
        interleave_w(nc.scalar.copy, V, 2, ROW_TILES, stage_b)
        products(V, 1, range(CHUNKS))

        def gather_u(j, first, count, dest):
            nc.vector.tensor_copy(dest, uv[U][j][:].indirect(entries(lea, first, count)))

        def gather_v(j, first, count, from_u):
            picked = uv[V][j][:].indirect(entries(inn, first, count))
            nc.vector.tensor_tensor(wide[j][:, first : first + count], picked, from_u, ALU.add)

        def gather_half(j, h, from_u):
            both = wide[j][:, h * HALF : (h + 1) * HALF]
            gather_u(j, h * HALF, HALF, from_u)
            nc.vector.tensor_copy(both, uv[V][j][:].indirect(entries(inn, h * HALF, HALF)))
            nc.gpsimd.tensor_tensor(both, both, from_u, ALU.add)

        def ring(j, h):
            return early[(2 * j + h) % PLANES][:, 0:HALF]

        def pair_sums_on_tensor(j, blocks):
            width = blocks * P
            for n in range(2):
                for b in range(blocks):
                    first = (n * blocks + b) * 2 * P
                    for odd in range(2):
                        nc.tensor.matmul(
                            banks[6 + n][:, b * P : (b + 1) * P],
                            wide[j][:, first + odd : first + 2 * P : 2],
                            ident[:],
                            start=(odd == 0),
                            stop=(odd == 1),
                            is_transpose=True,
                        )
                nc.scalar.copy(turned[n][:, 0:width], banks[6 + n][:, 0:width])
            for n in range(2):
                sums = result[(2 * j + n) % 4][:, 0:width]
                for b in range(blocks):
                    cols = slice(b * P, (b + 1) * P)
                    nc.tensor.transpose(banks[4 + n][:, cols], turned[n][:, cols], ident[:])
                nc.scalar.copy(sums, banks[4 + n][:, 0:width])
                nc.sync.dma_start(out[j * P : (j + 1) * P, n * width : (n + 1) * width], sums)

        whole = NODES // (2 * P)
        for h in range(2):
            gather_half(0, h, ring(0, h))
        quantise_w(U, 2, ROW_TILES, stage_a)
        quantise_w(V, 2, ROW_TILES, stage_b)
        gather_half(1, 0, stage.bitcast(F32))
        gather_half(1, 1, ring(1, 1))
        for j in (0, 1):
            pair_sums_on_tensor(j, whole)
            products(U, j + 2, range(CHUNKS))
            products(V, j + 2, range(CHUNKS))
        for h in range(2):
            gather_half(2, h, ring(2, h))
        pair_sums_on_tensor(2, whole)

        for h in range(2):
            gather_u(LAST_TILE, h * HALF, HALF, last[:, h * HALF : (h + 1) * HALF])
        quarter = EDGES // 4

        def pair_sums_on_vector(q):
            both = wide[LAST_TILE][:, q * quarter : (q + 1) * quarter]
            nodes = slice(q * quarter // 2, (q + 1) * quarter // 2)
            nc.vector.tensor_tensor(tail[:, nodes], both[:, 0::2], both[:, 1::2], ALU.add)
            nc.sync.dma_start(out[LAST_TILE * P :, nodes], tail[:, nodes])

        for q in range(4):
            gather_v(LAST_TILE, q * quarter, quarter, last[:, q * quarter : (q + 1) * quarter])
            if q == 0:
                pair_sums_on_tensor(LAST_TILE, 1)
            if q >= 2:
                pair_sums_on_vector(q - 1)
        pair_sums_on_vector(3)
